import numpy as np, ml_dtypes
CORES = [25,29,65,69,153,157,193,197]
N = 8
BF = ml_dtypes.bfloat16
def gentries(a):
    return np.ascontiguousarray(a.reshape(8, 16, -1).transpose(0, 2, 1)).reshape(8, -1)
def gtable(e):
    e = np.asarray(e); return np.ascontiguousarray(e.reshape(8, -1, 16).transpose(0, 2, 1)).reshape(128, -1).astype(np.int32)
M, B, H, ST = 192, 8, 5, 3
W = M * B
def parts(rng):
    c = np.minimum((W * np.exp2(-5 * rng.random((N, 8, 1, W))) * rng.random((N, 8, 16, W))).astype(np.int64), W - 1)
    a = np.exp2(5 * rng.random((N, 8, 16, 1))); q = rng.choice(np.array([1, 1, 1, 16, 256]), (N, 8, 16, 1))
    l = np.minimum((W * rng.random((N, 8, 16, W)) ** a).astype(np.int64), W - 1) & -q
    gap = np.minimum((W * (0.1 + 0.8 * rng.random((N, 8, 1, M))) * (0.5 + rng.random((N, 8, 16, M)))).astype(np.int64), W - 1)
    return c, l, gap, rng.integers(0, B, (N, 8, M))
def pack(c, l, gap, cur):
    return {"ck": np.ascontiguousarray(c.reshape(N, 128, W)).astype(np.int32), "la": np.ascontiguousarray(l.reshape(N, 128, W)).astype(np.int32),
            "gap": np.ascontiguousarray(gap.reshape(N, 128, M)).astype(np.int32), "cu": np.stack([gtable(a) for a in cur])}
def setup_inputs(rng):
    return pack(*parts(rng))
def setup_inputs_ties(rng):
    c, l, gap, cur = parts(rng); c = c & -64; gap = gap & -64; l = l & -64
    kind = rng.integers(0, 4, (N, 8, 16, 1)); kind[:, :, :4, 0] = np.arange(4)
    few = np.take_along_axis(rng.integers(0, W, (N, 8, 16, 4)), rng.integers(0, kind + 1, (N, 8, 16, W)), 3)
    l[:, ::2] = few[:, ::2]
    gap = np.where((rng.random((N, 8, 1, M)) < 0.25) & (rng.random((N, 8, 16, M)) < 0.2), 0, gap)
    return pack(c, l, gap, cur)
def setup_inputs_alike(rng):
    c, l, gap, cur = parts(rng)
    c[:, ::2] = np.maximum(c[:, ::2, :1], 16); c[:, ::2, :, 0] = rng.integers(0, 16, (N, 4, 16))
    c[:, 1::2] = rng.choice(np.array([3, W // 3, W // 2, W - 1]), (N, 4, 16, W))
    cur[:, :, 0] = 0; gap[:, :, :, 0] = 0
    return pack(c, l, gap, cur)
def setup_inputs_ends(rng):
    c, l, gap, cur = parts(rng)
    c[:, 0:4] = rng.choice(np.array([0, 1, W - 2, W - 1]), (N, 4, 16, W))
    l[:, 2:6] = rng.choice(np.array([0, 1, W - 2, W - 1]), (N, 4, 16, W))
    gap[:, 1:7] = rng.choice(np.array([0, 1, W - 1]), (N, 6, 16, M))
    cur = rng.choice(np.array([0, B - 1]), (N, 8, M))
    return pack(c, l, gap, cur)
def setup_inputs_count(rng):
    c, l, gap, cur = parts(rng); c = np.maximum(c, 1)
    n = rng.choice(np.array([0, H - 1, H, H + 1, 16]), (N, 8, 1, M)); g = rng.permutation(8)
    n[:, g[0]] = 16; n[:, g[1]] = 0; n[:, g[2], 0, :5] = np.array([0, H - 1, H, H + 1, 16])
    cur[:, g[0], :B] = np.arange(B)
    n[0::2, g[3]] = 16; n[1::2, g[3]] = 0
    n[:, g[4]] = 16; l[:, g[4]] = l[:, g[4], :, :1].copy(); c[:, g[4], :, 0] = 0
    cur[:, g[4], 0] = 1; cur[:, g[4], 1:9] = (2 * np.arange(N)[:, None] + np.arange(8)) & (B - 1)
    gap = np.where(np.argsort(rng.random((N, 8, 16, M)), axis=2) < n, 0, W - 1)
    return pack(c, l, gap, cur)
def setup_inputs_spread(rng):
    c, l, gap, cur = parts(rng); e = np.log2(W)
    c = np.minimum((np.exp2(e * rng.random((N, 8, 1, W))) * rng.random((N, 8, 16, W))).astype(np.int64), W - 1)
    l = np.minimum(np.exp2(e * rng.random((N, 8, 16, W)) ** (2 * rng.random((N, 8, 16, 1)))).astype(np.int64), W - 1)
    gap = np.minimum((np.exp2(e * (1 - rng.random((N, 8, 1, M)) ** 3)) * rng.random((N, 8, 16, M))).astype(np.int64), W - 1)
    return pack(c, l, gap, cur)
def check_inputs(d):
    bad = []
    for k, hi in (("ck", W - 1), ("la", W - 1), ("gap", W - 1), ("cu", B - 1)):
        if np.min(d[k]) < 0 or np.max(d[k]) > hi: bad.append("range of " + k)
    return bad
def columns(t, x):
    return np.take_along_axis(t, np.swapaxes(x, 2, 3).reshape(N, 8, 1, 16 * M), 3).reshape(N, 8, 16, M, 16)
def reference(ck, la, gap, cu):
    C = ck.astype(np.int64).reshape(N, 8, 16, W); L = la.astype(np.int64).reshape(N, 8, 16, W); G = gap.astype(np.int64).reshape(N, 8, 16, M)
    cur = np.stack([gentries(a) for a in cu]).astype(np.int64); first = B * np.arange(M)
    I = np.take_along_axis(C, (first + cur)[:, :, None, :], 3); T = I + G
    for step in range(ST):
        A = columns(L, I); top = np.max(A, axis=4, keepdims=True)
        s = np.max(np.where(A < top, A, 0), axis=4)
        I = np.maximum(I, np.max(columns(C, s), axis=4))
        out = np.add.reduce((I >= T).astype(np.int64), axis=2) >= H
        hit = (np.arange(B) == cur[..., None]) & out[..., None]
        C = np.where(hit[:, :, None], I[..., None], C.reshape(N, 8, 16, M, B)).reshape(N, 8, 16, W)
        cur = np.where(out, (cur + 1) & (B - 1), cur)
        new = np.take_along_axis(C, (first + cur)[:, :, None, :], 3)
        T = np.where(out[:, :, None], new + G, T); I = np.where(out[:, :, None], new, I)
        I, T, G, cur = np.roll(I, 1, axis=0), np.roll(T, 1, axis=0), np.roll(G, 1, axis=0), np.roll(cur, 1, axis=0)
    return {"yi": I.reshape(N, 128, M).astype(np.float32), "yc": np.stack([gtable(a) for a in cur]).astype(np.float32)}

@@ -1,0 +1,495 @@
+from concourse.mybir import AluOpType, ActivationFunctionType
+
+M, B, H, ST, W = 192, 8, 5, 3, 1536
+SIZES = [96, 96]
+K = len(SIZES)
+OFF = [sum(SIZES[:k]) for k in range(K)]
+DUMP = M
+BIG = 2048.0
+CB = 4096.0
+HALF = -(H - 0.5) / 16.0
+VL0 = [0] * K
+VL = [0] * K
+VG = [0] * K
+ORDER = ["L0", "L1", "P0", "V0", "N0", "G0", "P1", "V1", "N1", "Z0", "F0", "G1", "X0", "Z1", "F1", "X1"]
+
+E = 16 * M
+MW = [2 * n + n // 16 for n in SIZES]
+MO = [sum(MW[:k]) for k in range(K)]
+MT = sum(MW)
+SCRATCH = {
+    "C": ("sbuf", [128, DUMP + W], "int32"),
+    "L": ("sbuf", [128, W], "int32"),
+    "cus": ("sbuf", [128, 12], "int32"),
+    "gaps": ("sbuf", [128, M], "int32"),
+    "gapf": ("sbuf", [128, M], "float16"),
+    "gapL": ("sbuf", [128, M], "float16"),
+    "RM": ("sbuf", [128, 16 * max(SIZES)], "bfloat16"),
+    "EX": ("sbuf", [128, 512], "float16"),
+    "ID": ("sbuf", [128, 128], "float16"),
+    "N4": ("sbuf", [128, 128], "float16"),
+    "NI": ("sbuf", [128, 128], "float16"),
+    "BP": ("sbuf", [128, 128], "float16"),
+    "BN": ("sbuf", [128, 128], "float16"),
+    "HB": ("sbuf", [128, 128], "float16"),
+    "DM": ("sbuf", [128, M], "float32"),
+    "i1": ("sbuf", [128, 512], "int32"),
+    "i2": ("sbuf", [128, 128], "int32"),
+    "i3": ("sbuf", [128, 128], "int32"),
+    "i4": ("sbuf", [128, M], "int32"),
+    "i5": ("sbuf", [128, 12], "int32"),
+    "i6": ("sbuf", [128, 12], "int32"),
+    "b8": ("sbuf", [128, 12], "float32"),
+    "b5": ("sbuf", [128, 12], "float16"),
+    "b188": ("sbuf", [128, 12], "float16"),
+    "cd": ("sbuf", [128, 12], "float32"),
+    "I0f": ("sbuf", [128, 12], "float32"),
+    "I0u": ("sbuf", [128, 12], "uint16"),
+    "cuf": ("sbuf", [128, 12], "float16"),
+    "Io0": ("sbuf", [128, M], "float16"),
+    "T0": ("sbuf", [128, M], "float16"),
+    "J0": ("sbuf", [128, M], "uint16"),
+    "wo": ("sbuf", [128, 12 * ST], "float32"),
+    "ou": ("sbuf", [128, 12 * ST], "uint16"),
+    "Fy": ("sbuf", [128, 12], "float32"),
+    "oFy": ("sbuf", [128, 12], "float32"),
+    "oFq": ("sbuf", [128, 12], "float32"),
+    "J": ("sbuf", [128, ST * M], "uint16"),
+    "oJ": ("sbuf", [128, ST * M], "uint16"),
+    "Ms": ("sbuf", [128, ST * MT], "float16"),
+    "oMs": ("sbuf", [128, ST * MT], "float16"),
+    "F": ("sbuf", [128, M], "float32"),
+    "oF": ("sbuf", [128, M], "float32"),
+    "xp": ("psum", [128, E], "float32"),
+    "tp": ("psum", [128, 512], "float32"),
+    "wp": ("psum", [128, 512], "float32"),
+}
+for _n in ("A", "P", "V", "S", "BB", "Z"):
+    SCRATCH[_n] = ("sbuf", [128, ST * E], "float16")
+for _n, _d in (("su", "uint16"), ("RR", "float16"), ("Rg", "float16"), ("In", "float16"), ("GE", "float16"),
+               ("m1", "float16"), ("t1", "float16"), ("DD", "float16"), ("DS", "float16")):
+    SCRATCH[_n] = ("sbuf", [128, ST * M], _d)
+for _n, _d in (("sg", "float16"), ("sh", "float16"), ("Ru", "uint16")):
+    SCRATCH[_n] = ("sbuf", [128, ST * 12], _d)
+SCRATCH["tT"] = ("sbuf", [128, ST * K * 128], "float16")
+SEMAPHORES = ["v", "a", "p", "gq", "ls", "lcu", "lck0", "lck1", "lla", "lgap", "agap", "aFy", "st"]
+for _k in range(K):
+    for _s in range(1, ST):
+        SEMAPHORES += ["aJ%d_%d" % (_s, _k), "aM%d_%d" % (_s, _k)]
+    SEMAPHORES += ["aF%d" % _k]
+
+MSGS = [("gapL", 0, M, "agap", 1)]
+for _s in range(1, ST):
+    for _k in range(K):
+        MSGS += [("J", _s * M + OFF[_k], _s * M + OFF[_k] + SIZES[_k], "aJ%d_%d" % (_s, _k), 0),
+                 ("Ms", _s * MT + MO[_k], _s * MT + MO[_k] + MW[_k], "aM%d_%d" % (_s, _k), 1)]
+MSGS += [("F", OFF[_k], OFF[_k] + SIZES[_k], "aF%d" % _k, 0) for _k in range(K)] + [("Fy", 0, 12, "aFy", 1)]
+MSG = {m[3]: m for m in MSGS}
+
+
+def lanes(topo, cores, src, dst):
+    if topo.may_write(src, dst):
+        return [dst, dst]
+    own = [c for c in topo.cores_of(src) if c not in cores and topo.may_write(c, dst)]
+    own.sort(key=lambda c: (topo.die(c) != topo.die(src), c))
+    return [own[0], own[1 % len(own)]]
+
+
+def nbits(m):
+    return bin(m).count("1")
+
+
+def rank_program(g, core, T, topo):
+    cores = list(T.cores)
+    n_ranks = len(cores)
+    sem = T.sem
+    rank = T.rank_of(core)
+
+    def send(dst, src_name, sname):
+        name, c0, c1 = MSG[sname][:3]
+        rid, pid = topo.addr(dst, core)
+        m = topo.mask(core, dst)
+        g.remote_dma(T[name][:, c0:c1], T[src_name][:, c0:c1], sem[sname], sem.ls, pid, rid, m)
+        return nbits(m)
+
+    if rank is None:
+        total = 0
+        for r in range(n_ranks):
+            src, dst = cores[r], cores[(r + 1) % n_ranks]
+            way = lanes(topo, cores, src, dst)
+            if core not in way:
+                continue
+            for name, c0, c1, sname, lane in MSGS:
+                if way[lane] == core:
+                    g.wait_ge(sem[sname], nbits(topo.mask(src, core)))
+                    total += send(dst, name, sname)
+        if total:
+            g.wait_ge(sem.ls, total)
+        return
+
+    nxt, prv = cores[(rank + 1) % n_ranks], cores[(rank - 1) % n_ranks]
+    way = lanes(topo, cores, core, nxt)
+    inway = lanes(topo, cores, prv, core)
+    arrives = [nbits(topo.mask(prv if w == core else w, core)) for w in inway]
+    sent = [0]
+
+    queues = {"v": (g.vector, "v"), "a": (g.scalar, "a"), "p": (g.tensor, "p"), "g": (g, "gq"), "s": (g.sync, "st")}
+    count = {q: 0 for q in queues}
+    seen = {q: {} for q in queues}
+    wrote, readers, banks = {}, {}, {}
+
+    def wait(q, deps):
+        need = {}
+        for s, val in deps:
+            need[s] = max(need.get(s, 0), val)
+        for s in sorted(need):
+            if seen[q].get(s, 0) < need[s]:
+                queues[q][0].wait_ge(sem[s], need[s])
+                seen[q][s] = need[s]
+
+    def op(q, R, Wk, call, bank=()):
+        d = [wrote[k] for k in R if k in wrote]
+        for k in Wk:
+            if k in wrote:
+                d.append(wrote[k])
+            d += readers.get(k, [])
+        for b in bank:
+            d += [t for qq, t in banks.get(b, {}).items() if qq != q]
+        wait(q, d)
+        s = queues[q][1]
+        call().then_inc(sem[s], 1)
+        count[q] += 1
+        tok = (s, count[q])
+        for k in R:
+            readers.setdefault(k, []).append(tok)
+        for k in Wk:
+            wrote[k] = tok
+            readers[k] = []
+        for b in bank:
+            banks.setdefault(b, {})[q] = tok
+
+    def load(eng, name, s, out, in_):
+        eng.dma_start(out, in_).then_inc(sem[s], 16)
+        wrote[name] = (s, 16)
+
+    def push(src_name, sname, R):
+        wait("g", [wrote[k] for k in R])
+        sent[0] += send(way[MSG[sname][4]], src_name, sname)
+
+    def landed(name, sname):
+        wrote[name] = (sname, arrives[MSG[sname][4]])
+
+    AO, AF = AluOpType, ActivationFunctionType
+    v, te, sc = g.vector, g.tensor, g.scalar
+
+    def ts(out, in0, s1, o0, s2=None, o1=None):
+        if o1 is None:
+            return lambda: v.tensor_scalar(out, in0, s1, None, o0)
+        return lambda: v.tensor_scalar(out, in0, s1, s2, o0, o1)
+
+    def tt(out, a, b, o):
+        return lambda: v.tensor_tensor(out, a, b, o)
+
+    def tc(out, in_):
+        return lambda: v.tensor_copy(out, in_)
+
+    def mm(out, lhsT, rhs, start=True, stop=True):
+        return lambda: te.matmul(out, lhsT, rhs, start, stop)
+
+    def scan(out, mask, data):
+        return lambda: v.tensor_tensor_scan(out, mask, data, 0.0, AO.mult, AO.max)
+
+    def act(out, in_):
+        return lambda: sc.activation(out, in_, AF.Copy)
+
+    n0 = 8 * SIZES[0]
+    load(g.scalar, "cus", "lcu", T.cus[:], T.cu[:])
+    load(g.sync, ("C", 0), "lck0", T.C[:, DUMP:DUMP + n0], T.ck[:, 0:n0])
+    load(g.sync, "L", "lla", T.L[:], T.la[:])
+    load(g.sync, "gaps", "lgap", T.gaps[:], T.gap[:])
+    load(g.sync, ("C", 1), "lck1", T.C[:, DUMP + n0:DUMP + W], T.ck[:, n0:W])
+
+    op("g", [], ["i5"], lambda: g.iota(T.i5[:], [[0, 12]], 0, 8))
+    op("g", [], ["i6"], lambda: g.iota(T.i6[:], [[128, 12]], 0, 0))
+    op("g", [], ["i2"], lambda: g.iota(T.i2[:], [[1, 128]], 0, -1))
+    op("g", [], ["i1"], lambda: g.iota(T.i1[:], [[1, 512]], 0, -16))
+    op("g", [], ["i3"], lambda: g.iota(T.i3[:], [[16, 8], [0, 16]], 15, -1))
+    op("g", [], ["i4"], lambda: g.iota(T.i4[:], [[1, M]], 0, -1))
+
+    op("v", ["i5"], ["i5"], ts(T.i5[:], T.i5[:], 127, AO.bitwise_and))
+    op("v", [], ["RM"], lambda: v.memset(T.RM[:], 1.0))
+    op("v", ["i5", "i6"], ["b8"], tt(T.b8[:], T.i5[:], T.i6[:], AO.add))
+    op("v", [], ["RM"], lambda: v.memset(T.RM[:, 0:16 * max(SIZES):16], 0.0))
+    op("v", ["b8", "cus"], ["I0f"], tt(T.I0f[:], T.b8[:], T.cus[:], AO.add))
+    op("v", ["I0f"], ["I0u"], tc(T.I0u[:], T.I0f[:]))
+    op("v", ["cus"], ["cuf"], tc(T.cuf[:], T.cus[:]))
+    op("v", ["i2"], ["ID"], ts(T.ID[:], T.i2[:], 0.0, AO.is_equal))
+    op("v", ["i2"], ["NI"], ts(T.NI[:], T.i2[:], 0.0, AO.is_equal, -BIG, AO.mult))
+    op("v", ["i1"], ["i1"], ts(T.i1[:], T.i1[:], 511, AO.bitwise_and))
+    op("v", ["i3"], ["i3"], ts(T.i3[:], T.i3[:], 4, AO.arith_shift_right))
+    op("v", ["i4"], ["i4"], ts(T.i4[:], T.i4[:], 15, AO.bitwise_and))
+    op("v", ["i1"], ["EX"], ts(T.EX[:], T.i1[:], 16.0, AO.is_lt, BIG, AO.mult))
+    op("v", ["i2"], ["N4"], ts(T.N4[:], T.i2[:], 0.0, AO.is_equal, -4.0, AO.mult))
+    op("v", ["i3"], ["BP"], ts(T.BP[:], T.i3[:], 0.0, AO.is_equal, CB, AO.mult))
+    op("v", ["i3"], ["BN"], ts(T.BN[:], T.i3[:], 0.0, AO.is_equal, -CB, AO.mult))
+    op("v", ["i2"], ["HB"], ts(T.HB[:], T.i2[:], 0.0, AO.mult, HALF, AO.add))
+    op("v", ["i4"], ["DM"], ts(T.DM[:], T.i4[:], 0.0, AO.is_gt, 1.0e6, AO.mult))
+    op("v", ["b8"], ["b5"], ts(T.b5[:], T.b8[:], -3.0, AO.add))
+    op("v", ["b8"], ["b188"], ts(T.b188[:], T.b8[:], float(DUMP - 4), AO.add))
+    op("v", ["b8"], ["cd"], ts(T.cd[:], T.b8[:], 0.125, AO.mult))
+
+    allC = [("C", 0), ("C", 1)]
+
+    def cl(s, k):
+        return s * 12 + OFF[k] // 16, s * 12 + (OFF[k] + SIZES[k]) // 16
+
+    def sl(name, s, k):
+        return T[name][:, s * M + OFF[k]:s * M + OFF[k] + SIZES[k]]
+
+    def big(name, s, k, a=0, b=None):
+        o = s * E + 16 * OFF[k]
+        return T[name][:, o + 16 * a:o + 16 * (SIZES[k] if b is None else b)]
+
+    def lasts(name, s, k):
+        o = s * E + 16 * OFF[k]
+        return T[name][:, o + 15:o + 16 * SIZES[k]:16]
+
+    def xb(k, m, a, b):
+        o = 16 * OFF[k] + 512 * m
+        return T.xp[:, o + a:o + b]
+
+    def ideal(s, k):
+        n = SIZES[k]
+        if s == 0:
+            return T.Io0[:, OFF[k]:OFF[k] + n], ("Io", k)
+        o = s * MT + MO[k]
+        return T.Ms[:, o:o + n], ("M", s, k)
+
+    def bound(s, k):
+        n = SIZES[k]
+        if s == 0:
+            return T.T0[:, OFF[k]:OFF[k] + n], ("T0", k)
+        o = s * MT + MO[k] + n
+        return T.Ms[:, o:o + n], ("M", s, k)
+
+    def place(s, k):
+        n = SIZES[k]
+        if s == 0:
+            return T.cuf[:, OFF[k] // 16:(OFF[k] + n) // 16], "cuf"
+        o = s * MT + MO[k] + 2 * n
+        return T.Ms[:, o:o + n // 16], ("M", s, k)
+
+    def gather(q, R, Wk, out, win, off):
+        if q == "v":
+            op("v", R, Wk, tc(out, win.indirect(off)))
+        else:
+            op("a", R, Wk, act(out, win.indirect(off)))
+
+    def first(k):
+        o, n = OFF[k], SIZES[k]
+        keys = [("C", 0)] if k == 0 else allC
+        gather("a", ["I0u"] + keys, [("Io", k)], T.Io0[:, o:o + n], T.C[:, DUMP:DUMP + 8 * (o + n)],
+               T.I0u[:, o // 16:(o + n) // 16])
+        op("v", [("Io", k)], [("J", 0, k)], tc(T.J0[:, o:o + n], T.Io0[:, o:o + n]))
+
+    def stL(s, k):
+        n = SIZES[k]
+        if s == 0:
+            J = T.J0[:, OFF[k]:OFF[k] + n]
+            j0 = OFF[k]
+        else:
+            landed(("J", s, k), "aJ%d_%d" % (s, k))
+            j0 = s * M + OFF[k]
+        J = T.J0 if s == 0 else T.J
+        nv = (VL0 if s == 0 else VL)[k]
+        na = n - nv
+        if na:
+            gather("a", [("J", s, k), "L"], [("A", s, k, 0)], big("A", s, k, 0, na), T.L[:], J[:, j0:j0 + na])
+        if nv:
+            gather("v", [("J", s, k), "L"], [("A", s, k, 1)], big("A", s, k, na, n), T.L[:], J[:, j0 + na:j0 + n])
+
+    def akeys(s, k):
+        return [("A", s, k, 0), ("A", s, k, 1)]
+
+    def stP(s, k):
+        n = SIZES[k]
+        op("v", akeys(s, k) + ["RM"], [("P", s, k)], scan(big("P", s, k), T.RM[:, 0:16 * n], big("A", s, k)))
+        for m in range(n // 32):
+            op("p", akeys(s, k) + ["NI"], [("X", s, k, m)],
+               mm(xb(k, m, 0, 512), T.NI[:], big("A", s, k, 32 * m, 32 * m + 32), True, False), [(k, m)])
+        op("p", [("P", s, k), "ID"], [("tp", s, k)], mm(T.tp[0:n, 0:128], lasts("P", s, k), T.ID[:]), ["tp"])
+        o = 128 * (s * K + k)
+        op("a", [("tp", s, k)], [("tT", s, k)], act(T.tT[0:n, o:o + 128], T.tp[0:n, 0:128]), ["tp"])
+        for m in range(n // 32):
+            op("p", [("tT", s, k), "EX"], [("X", s, k, m)],
+               mm(xb(k, m, 0, 512), T.tT[32 * m:32 * m + 32, o:o + 128], T.EX[32 * m:32 * m + 32, :], False, True),
+               [(k, m)])
+
+    def stV(s, k):
+        n = SIZES[k]
+        for m in range(n // 32):
+            op("v", akeys(s, k) + [("X", s, k, m)], [("V", s, k, m)],
+               tt(big("V", s, k, 32 * m, 32 * m + 32), xb(k, m, 0, 512), big("A", s, k, 32 * m, 32 * m + 32), AO.min),
+               [(k, m)])
+        op("v", [("V", s, k, m) for m in range(n // 32)] + ["RM"], [("S", s, k)],
+           scan(big("S", s, k), T.RM[:, 0:16 * n], big("V", s, k)))
+        op("v", [("S", s, k)], [("su", s, k)], tc(sl("su", s, k), lasts("S", s, k)))
+
+    def stN(s, k):
+        n = SIZES[k]
+        q = n // 16
+        c0, c1 = cl(s, k)
+        if s > 0:
+            landed(("M", s, k), "aM%d_%d" % (s, k))
+        y, yk = place(s, k)
+        sg, sh = T.sg[:, c0:c1], T.sh[:, c0:c1]
+        op("a", [yk], [("sg", s, k)], lambda: sc.activation(sg, y, AF.Sign, bias=-6.5))
+        op("a", [yk], [("sh", s, k)], lambda: sc.activation(sh, y, AF.Sign, bias=-7.5))
+        b = [(k, 1)]
+        p0 = 2 * n
+        b5 = T.b5[:, OFF[k] // 16:OFF[k] // 16 + q]
+        op("p", ["b5", "ID"], [("r", s, k)], mm(xb(k, 1, p0, p0 + q), T.ID[:], b5, True, False), b)
+        op("p", [yk], [("r", s, k)], mm(xb(k, 1, p0, p0 + q), T.ID[:], y, False, False), b)
+        op("p", [("sg", s, k), "N4"], [("r", s, k)], mm(xb(k, 1, p0, p0 + q), T.N4[:], sg, False, True), b)
+        I, ik = ideal(s, k)
+        op("p", [ik, "ID"], [("Ip", s, k)], mm(xb(k, 1, 0, n), T.ID[:], I), b)
+        if s == 0:
+            op("p", [ik, "ID"], [("Tp", s, k)], mm(xb(k, 1, n, 2 * n), T.ID[:], I, True, False), b)
+            op("p", ["gapf"], [("Tp", s, k)], mm(xb(k, 1, n, 2 * n), T.ID[:], T.gapf[:, OFF[k]:OFF[k] + n], False, True), b)
+        else:
+            t, tk = bound(s, k)
+            op("p", [tk, "ID"], [("Tp", s, k)], mm(xb(k, 1, n, 2 * n), T.ID[:], t), b)
+        op("v", [("r", s, k)], [("Ru", s, k)], tc(T.Ru[:, c0:c1], xb(k, 1, p0, p0 + q)), b)
+        if s < ST - 1:
+            w = T.wp[:, OFF[k] // 16:OFF[k] // 16 + q]
+            b188 = T.b188[:, OFF[k] // 16:OFF[k] // 16 + q]
+            op("p", ["b188", "ID"], [("w", s, k)], mm(w, T.ID[:], b188, True, False), ["wp"])
+            op("p", [yk], [("w", s, k)], mm(w, T.ID[:], y, False, False), ["wp"])
+            op("p", [("sh", s, k), "N4"], [("w", s, k)], mm(w, T.N4[:], sh, False, True), ["wp"])
+
+    def stG(s, k):
+        n = SIZES[k]
+        c0, c1 = cl(s, k)
+        nv = VG[k]
+        na = n - nv
+        win = T.C[:, DUMP:DUMP + W]
+        o = s * M + OFF[k]
+        if na:
+            gather("a", [("su", s, k)] + allC, [("B", s, k, 0)], big("BB", s, k, 0, na), win, T.su[:, o:o + na])
+        if nv:
+            gather("v", [("su", s, k)] + allC, [("B", s, k, 1)], big("BB", s, k, na, n), win, T.su[:, o + na:o + n])
+        gather("a", [("Ru", s, k)] + allC, [("RR", s, k)], sl("RR", s, k), win, T.Ru[:, c0:c1])
+
+    def stZ(s, k):
+        n = SIZES[k]
+        In, GE = sl("In", s, k), sl("GE", s, k)
+        op("v", [("B", s, k, 0), ("B", s, k, 1), "RM"], [("Z", s, k)],
+           scan(big("Z", s, k), T.RM[:, 0:16 * n], big("BB", s, k)))
+        op("v", [("Z", s, k), ("Ip", s, k)], [("In", s, k)], tt(In, xb(k, 1, 0, n), lasts("Z", s, k), AO.max), [(k, 1)])
+        op("v", [("In", s, k), ("Tp", s, k)], [("GE", s, k)], tt(GE, In, xb(k, 1, n, 2 * n), AO.is_ge), [(k, 1)])
+        b = [(k, 0)]
+        op("p", ["BP", "HB"], [("+", s, k)], mm(xb(k, 0, 0, n), T.BP[:], T.HB[:, 0:n], True, False), b)
+        op("p", [("GE", s, k)], [("+", s, k)], mm(xb(k, 0, 0, n), T.BP[:], GE, False, True), b)
+        op("p", ["BN", "HB"], [("-", s, k)], mm(xb(k, 0, n, 2 * n), T.BN[:], T.HB[:, 0:n], True, False), b)
+        op("p", [("GE", s, k)], [("-", s, k)], mm(xb(k, 0, n, 2 * n), T.BN[:], GE, False, True), b)
+        if s == 0:
+            t, tk = bound(s, k)
+            op("a", [("Tp", s, k)], [tk], act(t, xb(k, 1, n, 2 * n)), [(k, 1)])
+        if s < ST - 1:
+            gp, gk = (T.gapf, "gapf") if s == 0 else (T.gapL, "gapL")
+            if s == 1 and k == 0:
+                landed("gapL", "agap")
+            rg = xb(k, 1, 0, n)
+            op("p", [("RR", s, k), "ID"], [("Ip", s, k)], mm(rg, T.ID[:], sl("RR", s, k), True, False), [(k, 1)])
+            op("p", [gk, "ID"], [("Ip", s, k)], mm(rg, T.ID[:], gp[:, OFF[k]:OFF[k] + n], False, True), [(k, 1)])
+            op("a", [("Ip", s, k)], [("Rg", s, k)], act(sl("Rg", s, k), rg), [(k, 1)])
+
+    def pick(s, k, out, okeys, r, rk, i, ik, tmp, tkey):
+        n = SIZES[k]
+        b = [(k, 0)]
+        m2 = xb(k, 0, 2 * n, 3 * n)
+        op("v", [("+", s, k), rk], [(tkey, s, k)], tt(tmp, xb(k, 0, 0, n), r, AO.min), b)
+        op("v", [("-", s, k), ik], [("m2", s, k)], tt(m2, xb(k, 0, n, 2 * n), i, AO.min), b)
+        op("v", [(tkey, s, k), ("m2", s, k)], okeys, tt(out, m2, tmp, AO.max), b)
+
+    def stF(s, k):
+        n = SIZES[k]
+        if s < ST - 1:
+            o = (s + 1) * MT + MO[k]
+            out, key = T.oMs[:, o:o + n], ("oI", s + 1, k)
+        else:
+            out, key = T.oF[:, OFF[k]:OFF[k] + n], ("oF", k)
+        pick(s, k, out, [key], sl("RR", s, k), ("RR", s, k), sl("In", s, k), ("In", s, k), sl("m1", s, k), "m1")
+        if s < ST - 1:
+            op("v", [key], [("oJ", s + 1, k)], tc(sl("oJ", s + 1, k), out))
+            push("oJ", "aJ%d_%d" % (s + 1, k), [("oJ", s + 1, k)])
+        else:
+            push("oF", "aF%d" % k, [key])
+
+    def stX(s, k):
+        n = SIZES[k]
+        q = n // 16
+        D, DS = sl("DD", s, k), sl("DS", s, k)
+        op("v", [("+", s, k), "DM"], [("DD", s, k)], tt(D, xb(k, 0, 0, n), T.DM[:, OFF[k]:OFF[k] + n], AO.is_ge), [(k, 0)])
+        op("v", [("DD", s, k), "RM"], [("DS", s, k)], scan(DS, T.RM[:, 0:n], D))
+        y, yk = place(s, k)
+        o = s * M + OFF[k]
+        w = T.wp[:, 16 + OFF[k] // 16:16 + OFF[k] // 16 + q]
+        op("p", [yk, "ID"], [("y", s, k)], mm(w, T.ID[:], y, True, False), ["wp"])
+        op("p", [("DS", s, k)], [("y", s, k)], mm(w, T.ID[:], T.DS[:, o + 15:o + n:16], False, True), ["wp"])
+        if s < ST - 1:
+            o = (s + 1) * MT + MO[k]
+            op("a", [("y", s, k)], [("oy", s + 1, k)], act(T.oMs[:, o + 2 * n:o + 2 * n + q], w), ["wp"])
+            t, tk = bound(s, k)
+            pick(s, k, T.oMs[:, o + n:o + 2 * n], [("oT", s + 1, k)], sl("Rg", s, k), ("Rg", s, k), t, tk,
+                 sl("t1", s, k), "t1")
+            push("oMs", "aM%d_%d" % (s + 1, k), [("oI", s + 1, k), ("oT", s + 1, k), ("oy", s + 1, k)])
+
+    def tail(s):
+        ks = range(K)
+        wo, ou = T.wo[:, 12 * s:12 * s + 12], T.ou[:, 12 * s:12 * s + 12]
+        op("v", [("w", s, k) for k in ks] + [("DS", s, k) for k in ks], [("wo", s)],
+           tt(wo, T.wp[:, 0:12], T.DS[:, s * M + 15:s * M + M:16], AO.mult), ["wp"])
+        op("v", [("wo", s), "cd"], [("wo", s)], tt(wo, wo, T.cd[:], AO.max))
+        op("v", [("wo", s)], [("ou", s)], tc(ou, wo))
+        op("v", [("ou", s)] + [("In", s, k) for k in ks], allC,
+           tc(T.C[:, 0:DUMP + W].indirect(ou), T.In[:, s * M:s * M + M]))
+
+    stages = {"L": stL, "P": stP, "V": stV, "N": stN, "G": stG, "Z": stZ, "F": stF, "X": stX}
+
+    for k in range(K):
+        first(k)
+        if k == 0:
+            stL(0, 0)
+            op("v", ["gaps"], ["gapf"], tc(T.gapf[:], T.gaps[:]))
+    wait("g", [wrote["gapf"]])
+    rid, pid = topo.addr(way[1], core)
+    g.remote_dma(T.gapL[:], T.gapf[:], sem.agap, sem.ls, pid, rid, topo.mask(core, way[1]))
+    sent[0] += nbits(topo.mask(core, way[1]))
+    for s in range(ST):
+        for st in ORDER:
+            if s == 0 and st == "L0":
+                continue
+            stages[st[0]](s, int(st[1:]))
+        if s < ST - 1:
+            tail(s)
+    yk = [("y", ST - 1, k) for k in range(K)]
+    yp = T.wp[:, 16:28]
+    op("v", yk, ["oFq"], ts(T.oFq[:], yp, 8.0, AO.is_ge, -8.0, AO.mult), ["wp"])
+    op("v", yk + ["oFq"], ["oFy"], tt(T.oFy[:], yp, T.oFq[:], AO.add), ["wp"])
+    push("oFy", "aFy", ["oFy"])
+
+    total = 0
+    for k in range(K):
+        landed(("F", k), "aF%d" % k)
+        wait("s", [wrote[("F", k)]])
+        g.sync.dma_start(T.yi[:, OFF[k]:OFF[k] + SIZES[k]], T.F[:, OFF[k]:OFF[k] + SIZES[k]]).then_inc(sem.st, 16)
+        total += 16
+    landed("Fy", "aFy")
+    wait("s", [wrote["Fy"]])
+    g.sync.dma_start(T.yc[:], T.Fy[:]).then_inc(sem.st, 16)
+    total += 16
+    g.sync.wait_ge(sem.st, total)
+    g.wait_ge(sem.ls, sent[0])
+    for q, s in (("v", "v"), ("a", "a"), ("p", "p"), ("g", "gq")):
+        g.wait_ge(sem[s], count[q])

@@ -8,30 +8,36 @@ DUMP = M
 BIG = 2048.0
 CB = 4096.0
 HALF = -(H - 0.5) / 16.0
-VL0 = [0] * K
-VL = [0] * K
-VG = [0] * K
-ORDER = ["L0", "L1", "P0", "V0", "N0", "G0", "P1", "V1", "N1", "Z0", "F0", "G1", "X0", "Z1", "F1", "X1"]
+VL0 = [48, 0]
+VL = [48, 0]
+VG = [0, 0]
+ORDER = """
+0L0 0P0 0V01 0V02 0V00 0S0 0N0 0L1 0P1 0V10 0V11 0G0 0R0 0V12 0Z0 0S1 0F0 0X0 0N1 0G1 0R1 0Z1 0F1 1L0 1P0 0X1 0T
+1V01 1V00 1V02 1N0 1L1 1P1 1S0 1V10 1V11 1V12 1S1 1N1 1G0 1R0 1G1 1R1 1Z0 1F0 1X0 1Z1 1F1 1X1 2L0 2P0 1T
+2V01 2V02 2V00 2N0 2L1 2R0 2P1 2S0 2V10 2G0 2V11 2V12 2S1 2N1 2G1 2Z0 2F0 2R1 2Z1 2X0 2F1 2X1
+""".split()
 
 E = 16 * M
 MW = [2 * n + n // 16 for n in SIZES]
 MO = [sum(MW[:k]) for k in range(K)]
 MT = sum(MW)
+GO = [OFF[k] + OFF[k] // 8 for k in range(K)]
+GW = M + M // 8
+NM = max(SIZES)
 SCRATCH = {
     "C": ("sbuf", [128, DUMP + W], "int32"),
     "L": ("sbuf", [128, W], "int32"),
     "cus": ("sbuf", [128, 12], "int32"),
     "gaps": ("sbuf", [128, M], "int32"),
-    "gapf": ("sbuf", [128, M], "float16"),
-    "gapL": ("sbuf", [128, M], "float16"),
-    "RM": ("sbuf", [128, 16 * max(SIZES)], "bfloat16"),
+    "GB": ("sbuf", [128, ST * GW], "float16"),
+    "RM": ("sbuf", [128, 16 * NM], "bfloat16"),
     "EX": ("sbuf", [128, 512], "float16"),
     "ID": ("sbuf", [128, 128], "float16"),
     "N4": ("sbuf", [128, 128], "float16"),
     "NI": ("sbuf", [128, 128], "float16"),
     "BP": ("sbuf", [128, 128], "float16"),
     "BN": ("sbuf", [128, 128], "float16"),
-    "HB": ("sbuf", [128, 128], "float16"),
+    "HB": ("sbuf", [128, 2 * NM], "float16"),
     "DM": ("sbuf", [128, M], "float32"),
     "i1": ("sbuf", [128, 512], "int32"),
     "i2": ("sbuf", [128, 128], "int32"),
@@ -40,17 +46,17 @@ SCRATCH = {
     "i5": ("sbuf", [128, 12], "int32"),
     "i6": ("sbuf", [128, 12], "int32"),
     "b8": ("sbuf", [128, 12], "float32"),
-    "b5": ("sbuf", [128, 12], "float16"),
-    "b188": ("sbuf", [128, 12], "float16"),
     "cd": ("sbuf", [128, 12], "float32"),
     "I0f": ("sbuf", [128, 12], "float32"),
     "I0u": ("sbuf", [128, 12], "uint16"),
     "cuf": ("sbuf", [128, 12], "float16"),
     "Io0": ("sbuf", [128, M], "float16"),
-    "T0": ("sbuf", [128, M], "float16"),
     "J0": ("sbuf", [128, M], "uint16"),
     "wo": ("sbuf", [128, 12 * ST], "float32"),
     "ou": ("sbuf", [128, 12 * ST], "uint16"),
+    "sg": ("sbuf", [128, 24 * ST], "float16"),
+    "Ru": ("sbuf", [128, 12 * ST], "uint16"),
+    "Ry": ("sbuf", [128, 12], "float32"),
     "Fy": ("sbuf", [128, 12], "float32"),
     "oFy": ("sbuf", [128, 12], "float32"),
     "oFq": ("sbuf", [128, 12], "float32"),
@@ -60,31 +66,34 @@ SCRATCH = {
     "oMs": ("sbuf", [128, ST * MT], "float16"),
     "F": ("sbuf", [128, M], "float32"),
     "oF": ("sbuf", [128, M], "float32"),
+    "tT": ("sbuf", [128, ST * K * 128], "float16"),
     "xp": ("psum", [128, E], "float32"),
     "tp": ("psum", [128, 512], "float32"),
-    "wp": ("psum", [128, 512], "float32"),
 }
 for _n in ("A", "P", "V", "S", "BB", "Z"):
     SCRATCH[_n] = ("sbuf", [128, ST * E], "float16")
-for _n, _d in (("su", "uint16"), ("RR", "float16"), ("Rg", "float16"), ("In", "float16"), ("GE", "float16"),
-               ("m1", "float16"), ("t1", "float16"), ("DD", "float16"), ("DS", "float16")):
+for _n, _d in (("su", "uint16"), ("RR", "float16"), ("In", "float16"), ("GE", "float16"),
+               ("m1", "float16"), ("DD", "float16"), ("DS", "float16")):
     SCRATCH[_n] = ("sbuf", [128, ST * M], _d)
-for _n, _d in (("sg", "float16"), ("sh", "float16"), ("Ru", "uint16")):
-    SCRATCH[_n] = ("sbuf", [128, ST * 12], _d)
-SCRATCH["tT"] = ("sbuf", [128, ST * K * 128], "float16")
-SEMAPHORES = ["v", "a", "p", "gq", "ls", "lcu", "lck0", "lck1", "lla", "lgap", "agap", "aFy", "st"]
+SEMAPHORES = ["v", "a", "p", "gq", "ls", "lcu", "lck0", "lck1", "lla", "lgap", "agap1", "agap2", "aFy", "st"]
 for _k in range(K):
     for _s in range(1, ST):
         SEMAPHORES += ["aJ%d_%d" % (_s, _k), "aM%d_%d" % (_s, _k)]
     SEMAPHORES += ["aF%d" % _k]
 
-MSGS = [("gapL", 0, M, "agap", 1)]
-for _s in range(1, ST):
-    for _k in range(K):
-        MSGS += [("J", _s * M + OFF[_k], _s * M + OFF[_k] + SIZES[_k], "aJ%d_%d" % (_s, _k), 0),
-                 ("Ms", _s * MT + MO[_k], _s * MT + MO[_k] + MW[_k], "aM%d_%d" % (_s, _k), 1)]
-MSGS += [("F", OFF[_k], OFF[_k] + SIZES[_k], "aF%d" % _k, 0) for _k in range(K)] + [("Fy", 0, 12, "aFy", 1)]
-MSG = {m[3]: m for m in MSGS}
+MSG = {"agap1": ("GB", GW, 2 * GW, 1), "agap2": ("GB", 2 * GW, 3 * GW, 1), "aFy": ("Fy", 0, 12, 1)}
+for _k in range(K):
+    for _s in range(1, ST):
+        MSG["aJ%d_%d" % (_s, _k)] = ("J", _s * M + OFF[_k], _s * M + OFF[_k] + SIZES[_k], 0)
+        MSG["aM%d_%d" % (_s, _k)] = ("Ms", _s * MT + MO[_k], _s * MT + MO[_k] + MW[_k], 1)
+    MSG["aF%d" % _k] = ("F", OFF[_k], OFF[_k] + SIZES[_k], 0)
+ISSUE = ["agap1", "agap2"]
+for _t in ORDER:
+    if _t[1] == "F":
+        ISSUE.append("aJ%d_%s" % (int(_t[0]) + 1, _t[2]) if int(_t[0]) < ST - 1 else "aF" + _t[2])
+    if _t[1] == "X" and int(_t[0]) < ST - 1:
+        ISSUE.append("aM%d_%s" % (int(_t[0]) + 1, _t[2]))
+ISSUE.append("aFy")
 
 
 def lanes(topo, cores, src, dst):
@@ -105,11 +114,11 @@ def rank_program(g, core, T, topo):
     sem = T.sem
     rank = T.rank_of(core)
 
-    def send(dst, src_name, sname):
+    def send(dst, src_name, sname, back=0):
         name, c0, c1 = MSG[sname][:3]
         rid, pid = topo.addr(dst, core)
         m = topo.mask(core, dst)
-        g.remote_dma(T[name][:, c0:c1], T[src_name][:, c0:c1], sem[sname], sem.ls, pid, rid, m)
+        g.remote_dma(T[name][:, c0:c1], T[src_name][:, c0 - back:c1 - back], sem[sname], sem.ls, pid, rid, m)
         return nbits(m)
 
     if rank is None:
@@ -119,7 +128,8 @@ def rank_program(g, core, T, topo):
             way = lanes(topo, cores, src, dst)
             if core not in way:
                 continue
-            for name, c0, c1, sname, lane in MSGS:
+            for sname in ISSUE:
+                name, c0, c1, lane = MSG[sname]
                 if way[lane] == core:
                     g.wait_ge(sem[sname], nbits(topo.mask(src, core)))
                     total += send(dst, name, sname)
@@ -172,12 +182,12 @@ def rank_program(g, core, T, topo):
         eng.dma_start(out, in_).then_inc(sem[s], 16)
         wrote[name] = (s, 16)
 
-    def push(src_name, sname, R):
+    def push(src_name, sname, R, back=0):
         wait("g", [wrote[k] for k in R])
-        sent[0] += send(way[MSG[sname][4]], src_name, sname)
+        sent[0] += send(way[MSG[sname][3]], src_name, sname, back)
 
     def landed(name, sname):
-        wrote[name] = (sname, arrives[MSG[sname][4]])
+        wrote[name] = (sname, arrives[MSG[sname][3]])
 
     AO, AF = AluOpType, ActivationFunctionType
     v, te, sc = g.vector, g.tensor, g.scalar
@@ -219,7 +229,7 @@ def rank_program(g, core, T, topo):
     op("v", ["i5"], ["i5"], ts(T.i5[:], T.i5[:], 127, AO.bitwise_and))
     op("v", [], ["RM"], lambda: v.memset(T.RM[:], 1.0))
     op("v", ["i5", "i6"], ["b8"], tt(T.b8[:], T.i5[:], T.i6[:], AO.add))
-    op("v", [], ["RM"], lambda: v.memset(T.RM[:, 0:16 * max(SIZES):16], 0.0))
+    op("v", [], ["RM"], lambda: v.memset(T.RM[:, 0:16 * NM:16], 0.0))
     op("v", ["b8", "cus"], ["I0f"], tt(T.I0f[:], T.b8[:], T.cus[:], AO.add))
     op("v", ["I0f"], ["I0u"], tc(T.I0u[:], T.I0f[:]))
     op("v", ["cus"], ["cuf"], tc(T.cuf[:], T.cus[:]))
@@ -232,10 +242,14 @@ def rank_program(g, core, T, topo):
     op("v", ["i2"], ["N4"], ts(T.N4[:], T.i2[:], 0.0, AO.is_equal, -4.0, AO.mult))
     op("v", ["i3"], ["BP"], ts(T.BP[:], T.i3[:], 0.0, AO.is_equal, CB, AO.mult))
     op("v", ["i3"], ["BN"], ts(T.BN[:], T.i3[:], 0.0, AO.is_equal, -CB, AO.mult))
-    op("v", ["i2"], ["HB"], ts(T.HB[:], T.i2[:], 0.0, AO.mult, HALF, AO.add))
+    op("v", ["i2"], ["HB0"], ts(T.HB[:, 0:NM], T.i2[:, 0:NM], 0.0, AO.mult, HALF, AO.add))
+    op("v", ["i2"], ["HB1"], ts(T.HB[:, NM:2 * NM], T.i2[:, 0:NM], 0.0, AO.mult, -HALF, AO.add))
     op("v", ["i4"], ["DM"], ts(T.DM[:], T.i4[:], 0.0, AO.is_gt, 1.0e6, AO.mult))
-    op("v", ["b8"], ["b5"], ts(T.b5[:], T.b8[:], -3.0, AO.add))
-    op("v", ["b8"], ["b188"], ts(T.b188[:], T.b8[:], float(DUMP - 4), AO.add))
+    for k in range(K):
+        q, c = SIZES[k] // 16, OFF[k] // 16
+        o = GO[k] + SIZES[k]
+        op("v", ["b8"], [("b5", k)], ts(T.GB[:, o:o + q], T.b8[:, c:c + q], -3.0, AO.add))
+        op("v", ["b8"], [("b188", k)], ts(T.GB[:, o + q:o + 2 * q], T.b8[:, c:c + q], float(DUMP - 4), AO.add))
     op("v", ["b8"], ["cd"], ts(T.cd[:], T.b8[:], 0.125, AO.mult))
 
     allC = [("C", 0), ("C", 1)]
@@ -265,10 +279,10 @@ def rank_program(g, core, T, topo):
         o = s * MT + MO[k]
         return T.Ms[:, o:o + n], ("M", s, k)
 
-    def bound(s, k):
+    def base(s, k):
         n = SIZES[k]
         if s == 0:
-            return T.T0[:, OFF[k]:OFF[k] + n], ("T0", k)
+            return ideal(0, k)
         o = s * MT + MO[k] + n
         return T.Ms[:, o:o + n], ("M", s, k)
 
@@ -295,12 +309,10 @@ def rank_program(g, core, T, topo):
     def stL(s, k):
         n = SIZES[k]
         if s == 0:
-            J = T.J0[:, OFF[k]:OFF[k] + n]
-            j0 = OFF[k]
+            J, j0 = T.J0, OFF[k]
         else:
             landed(("J", s, k), "aJ%d_%d" % (s, k))
-            j0 = s * M + OFF[k]
-        J = T.J0 if s == 0 else T.J
+            J, j0 = T.J, s * M + OFF[k]
         nv = (VL0 if s == 0 else VL)[k]
         na = n - nv
         if na:
@@ -325,12 +337,13 @@ def rank_program(g, core, T, topo):
                mm(xb(k, m, 0, 512), T.tT[32 * m:32 * m + 32, o:o + 128], T.EX[32 * m:32 * m + 32, :], False, True),
                [(k, m)])
 
-    def stV(s, k):
+    def stV(s, k, m):
+        op("v", akeys(s, k) + [("X", s, k, m)], [("V", s, k, m)],
+           tt(big("V", s, k, 32 * m, 32 * m + 32), xb(k, m, 0, 512), big("A", s, k, 32 * m, 32 * m + 32), AO.min),
+           [(k, m)])
+
+    def stS(s, k):
         n = SIZES[k]
-        for m in range(n // 32):
-            op("v", akeys(s, k) + [("X", s, k, m)], [("V", s, k, m)],
-               tt(big("V", s, k, 32 * m, 32 * m + 32), xb(k, m, 0, 512), big("A", s, k, 32 * m, 32 * m + 32), AO.min),
-               [(k, m)])
         op("v", [("V", s, k, m) for m in range(n // 32)] + ["RM"], [("S", s, k)],
            scan(big("S", s, k), T.RM[:, 0:16 * n], big("V", s, k)))
         op("v", [("S", s, k)], [("su", s, k)], tc(sl("su", s, k), lasts("S", s, k)))
@@ -342,34 +355,34 @@ def rank_program(g, core, T, topo):
         if s > 0:
             landed(("M", s, k), "aM%d_%d" % (s, k))
         y, yk = place(s, k)
-        sg, sh = T.sg[:, c0:c1], T.sh[:, c0:c1]
-        op("a", [yk], [("sg", s, k)], lambda: sc.activation(sg, y, AF.Sign, bias=-6.5))
-        op("a", [yk], [("sh", s, k)], lambda: sc.activation(sh, y, AF.Sign, bias=-7.5))
+        o = 24 * s + OFF[k] // 8
+        op("a", [yk], [("sg", s, k)], lambda: sc.activation(T.sg[:, o:o + q], y, AF.Sign, bias=-6.5))
+        op("a", [yk], [("sh", s, k)], lambda: sc.activation(T.sg[:, o + q:o + 2 * q], y, AF.Sign, bias=-7.5))
         b = [(k, 1)]
         p0 = 2 * n
-        b5 = T.b5[:, OFF[k] // 16:OFF[k] // 16 + q]
-        op("p", ["b5", "ID"], [("r", s, k)], mm(xb(k, 1, p0, p0 + q), T.ID[:], b5, True, False), b)
-        op("p", [yk], [("r", s, k)], mm(xb(k, 1, p0, p0 + q), T.ID[:], y, False, False), b)
-        op("p", [("sg", s, k), "N4"], [("r", s, k)], mm(xb(k, 1, p0, p0 + q), T.N4[:], sg, False, True), b)
-        I, ik = ideal(s, k)
-        op("p", [ik, "ID"], [("Ip", s, k)], mm(xb(k, 1, 0, n), T.ID[:], I), b)
+        N = ("N", s, k)
         if s == 0:
-            op("p", [ik, "ID"], [("Tp", s, k)], mm(xb(k, 1, n, 2 * n), T.ID[:], I, True, False), b)
-            op("p", ["gapf"], [("Tp", s, k)], mm(xb(k, 1, n, 2 * n), T.ID[:], T.gapf[:, OFF[k]:OFF[k] + n], False, True), b)
+            I, ik = ideal(s, k)
+            gk = ("gb", k)
+            op("p", [ik, "ID"], [N], mm(xb(k, 1, 0, n), T.ID[:], I, True, False), b)
+            op("p", [ik, "ID"], [N], mm(xb(k, 1, n, p0), T.ID[:], I, False, False), b)
+            op("p", [yk, "ID"], [N], mm(xb(k, 1, p0, p0 + q), T.ID[:], y, False, False), b)
         else:
-            t, tk = bound(s, k)
-            op("p", [tk, "ID"], [("Tp", s, k)], mm(xb(k, 1, n, 2 * n), T.ID[:], t), b)
-        op("v", [("r", s, k)], [("Ru", s, k)], tc(T.Ru[:, c0:c1], xb(k, 1, p0, p0 + q)), b)
-        if s < ST - 1:
-            w = T.wp[:, OFF[k] // 16:OFF[k] // 16 + q]
-            b188 = T.b188[:, OFF[k] // 16:OFF[k] // 16 + q]
-            op("p", ["b188", "ID"], [("w", s, k)], mm(w, T.ID[:], b188, True, False), ["wp"])
-            op("p", [yk], [("w", s, k)], mm(w, T.ID[:], y, False, False), ["wp"])
-            op("p", [("sh", s, k), "N4"], [("w", s, k)], mm(w, T.N4[:], sh, False, True), ["wp"])
+            m = s * MT + MO[k]
+            gk = "GB%d" % s
+            if gk not in wrote:
+                landed(gk, "agap%d" % s)
+            op("p", [yk, "ID"], [N], mm(xb(k, 1, 0, p0 + q), T.ID[:], T.Ms[:, m:m + p0 + q], True, False), b)
+        op("p", [yk, "ID"], [N], mm(xb(k, 1, p0 + q, p0 + 2 * q), T.ID[:], y, False, False), b)
+        gs = s * GW + GO[k]
+        op("p", [gk, ("b5", k), ("b188", k)], [N],
+           mm(xb(k, 1, n, p0 + 2 * q), T.ID[:], T.GB[:, gs:gs + n + 2 * q], False, False), b)
+        op("p", [("sg", s, k), ("sh", s, k), "N4"], [N],
+           mm(xb(k, 1, p0, p0 + 2 * q), T.N4[:], T.sg[:, o:o + 2 * q], False, True), b)
+        op("v", [N], [("Ru", s, k)], tc(T.Ru[:, c0:c1], xb(k, 1, p0, p0 + q)), b)
 
     def stG(s, k):
         n = SIZES[k]
-        c0, c1 = cl(s, k)
         nv = VG[k]
         na = n - nv
         win = T.C[:, DUMP:DUMP + W]
@@ -378,39 +391,23 @@ def rank_program(g, core, T, topo):
             gather("a", [("su", s, k)] + allC, [("B", s, k, 0)], big("BB", s, k, 0, na), win, T.su[:, o:o + na])
         if nv:
             gather("v", [("su", s, k)] + allC, [("B", s, k, 1)], big("BB", s, k, na, n), win, T.su[:, o + na:o + n])
-        gather("a", [("Ru", s, k)] + allC, [("RR", s, k)], sl("RR", s, k), win, T.Ru[:, c0:c1])
+
+    def stR(s, k):
+        c0, c1 = cl(s, k)
+        gather("a", [("Ru", s, k)] + allC, [("RR", s, k)], sl("RR", s, k), T.C[:, DUMP:DUMP + W], T.Ru[:, c0:c1])
 
     def stZ(s, k):
         n = SIZES[k]
         In, GE = sl("In", s, k), sl("GE", s, k)
         op("v", [("B", s, k, 0), ("B", s, k, 1), "RM"], [("Z", s, k)],
            scan(big("Z", s, k), T.RM[:, 0:16 * n], big("BB", s, k)))
-        op("v", [("Z", s, k), ("Ip", s, k)], [("In", s, k)], tt(In, xb(k, 1, 0, n), lasts("Z", s, k), AO.max), [(k, 1)])
-        op("v", [("In", s, k), ("Tp", s, k)], [("GE", s, k)], tt(GE, In, xb(k, 1, n, 2 * n), AO.is_ge), [(k, 1)])
+        op("v", [("Z", s, k), ("N", s, k)], [("In", s, k)], tt(In, xb(k, 1, 0, n), lasts("Z", s, k), AO.max), [(k, 1)])
+        op("v", [("In", s, k), ("N", s, k)], [("GE", s, k)], tt(GE, In, xb(k, 1, n, 2 * n), AO.is_ge), [(k, 1)])
         b = [(k, 0)]
-        op("p", ["BP", "HB"], [("+", s, k)], mm(xb(k, 0, 0, n), T.BP[:], T.HB[:, 0:n], True, False), b)
-        op("p", [("GE", s, k)], [("+", s, k)], mm(xb(k, 0, 0, n), T.BP[:], GE, False, True), b)
-        op("p", ["BN", "HB"], [("-", s, k)], mm(xb(k, 0, n, 2 * n), T.BN[:], T.HB[:, 0:n], True, False), b)
-        op("p", [("GE", s, k)], [("-", s, k)], mm(xb(k, 0, n, 2 * n), T.BN[:], GE, False, True), b)
-        if s == 0:
-            t, tk = bound(s, k)
-            op("a", [("Tp", s, k)], [tk], act(t, xb(k, 1, n, 2 * n)), [(k, 1)])
-        if s < ST - 1:
-            gp, gk = (T.gapf, "gapf") if s == 0 else (T.gapL, "gapL")
-            if s == 1 and k == 0:
-                landed("gapL", "agap")
-            rg = xb(k, 1, 0, n)
-            op("p", [("RR", s, k), "ID"], [("Ip", s, k)], mm(rg, T.ID[:], sl("RR", s, k), True, False), [(k, 1)])
-            op("p", [gk, "ID"], [("Ip", s, k)], mm(rg, T.ID[:], gp[:, OFF[k]:OFF[k] + n], False, True), [(k, 1)])
-            op("a", [("Ip", s, k)], [("Rg", s, k)], act(sl("Rg", s, k), rg), [(k, 1)])
-
-    def pick(s, k, out, okeys, r, rk, i, ik, tmp, tkey):
-        n = SIZES[k]
-        b = [(k, 0)]
-        m2 = xb(k, 0, 2 * n, 3 * n)
-        op("v", [("+", s, k), rk], [(tkey, s, k)], tt(tmp, xb(k, 0, 0, n), r, AO.min), b)
-        op("v", [("-", s, k), ik], [("m2", s, k)], tt(m2, xb(k, 0, n, 2 * n), i, AO.min), b)
-        op("v", [(tkey, s, k), ("m2", s, k)], okeys, tt(out, m2, tmp, AO.max), b)
+        op("p", ["BP", "HB0", "HB1"], [("+", s, k)],
+           mm(xb(k, 0, 0, 2 * n), T.BP[:], T.HB[:, NM - n:NM + n], True, False), b)
+        op("p", [("GE", s, k)], [("+", s, k)], mm(xb(k, 0, 0, n), T.BP[:], GE, False, False), b)
+        op("p", [("GE", s, k), "BN"], [("+", s, k)], mm(xb(k, 0, n, 2 * n), T.BN[:], GE, False, True), b)
 
     def stF(s, k):
         n = SIZES[k]
@@ -419,7 +416,11 @@ def rank_program(g, core, T, topo):
             out, key = T.oMs[:, o:o + n], ("oI", s + 1, k)
         else:
             out, key = T.oF[:, OFF[k]:OFF[k] + n], ("oF", k)
-        pick(s, k, out, [key], sl("RR", s, k), ("RR", s, k), sl("In", s, k), ("In", s, k), sl("m1", s, k), "m1")
+        b = [(k, 0)]
+        m1, m2 = sl("m1", s, k), xb(k, 0, 2 * n, 3 * n)
+        op("v", [("+", s, k), ("RR", s, k)], [("m1", s, k)], tt(m1, xb(k, 0, 0, n), sl("RR", s, k), AO.min), b)
+        op("v", [("+", s, k), ("In", s, k)], [("m2", s, k)], tt(m2, xb(k, 0, n, 2 * n), sl("In", s, k), AO.min), b)
+        op("v", [("m1", s, k), ("m2", s, k)], [key], tt(out, m2, m1, AO.max), b)
         if s < ST - 1:
             op("v", [key], [("oJ", s + 1, k)], tc(sl("oJ", s + 1, k), out))
             push("oJ", "aJ%d_%d" % (s + 1, k), [("oJ", s + 1, k)])
@@ -429,54 +430,57 @@ def rank_program(g, core, T, topo):
     def stX(s, k):
         n = SIZES[k]
         q = n // 16
+        c = OFF[k] // 16
         D, DS = sl("DD", s, k), sl("DS", s, k)
-        op("v", [("+", s, k), "DM"], [("DD", s, k)], tt(D, xb(k, 0, 0, n), T.DM[:, OFF[k]:OFF[k] + n], AO.is_ge), [(k, 0)])
-        op("v", [("DD", s, k), "RM"], [("DS", s, k)], scan(DS, T.RM[:, 0:n], D))
-        y, yk = place(s, k)
-        o = s * M + OFF[k]
-        w = T.wp[:, 16 + OFF[k] // 16:16 + OFF[k] // 16 + q]
-        op("p", [yk, "ID"], [("y", s, k)], mm(w, T.ID[:], y, True, False), ["wp"])
-        op("p", [("DS", s, k)], [("y", s, k)], mm(w, T.ID[:], T.DS[:, o + 15:o + n:16], False, True), ["wp"])
+        b0 = [(k, 0)]
+        op("v", [("+", s, k), "DM"], [("DD", s, k)], tt(D, xb(k, 0, 0, n), T.DM[:, OFF[k]:OFF[k] + n], AO.is_ge), b0)
         if s < ST - 1:
             o = (s + 1) * MT + MO[k]
-            op("a", [("y", s, k)], [("oy", s + 1, k)], act(T.oMs[:, o + 2 * n:o + 2 * n + q], w), ["wp"])
-            t, tk = bound(s, k)
-            pick(s, k, T.oMs[:, o + n:o + 2 * n], [("oT", s + 1, k)], sl("Rg", s, k), ("Rg", s, k), t, tk,
-                 sl("t1", s, k), "t1")
+            m2 = xb(k, 0, 3 * n, 4 * n)
+            t, tk = base(s, k)
+            op("v", [("+", s, k), tk], [("m3", s, k)], tt(m2, xb(k, 0, n, 2 * n), t, AO.min), b0)
+        op("v", [("DD", s, k), "RM"], [("DS", s, k)], scan(DS, T.RM[:, 0:n], D))
+        if s < ST - 1:
+            op("v", [("m3", s, k), ("m1", s, k)], [("oT", s + 1, k)],
+               tt(T.oMs[:, o + n:o + 2 * n], m2, sl("m1", s, k), AO.max), b0)
+        y, yk = place(s, k)
+        os = s * M + OFF[k]
+        ls = T.DS[:, os + 15:os + n:16]
+        if s < ST - 1:
+            op("v", [("DS", s, k), yk], [("oy", s + 1, k)], tt(T.oMs[:, o + 2 * n:o + 2 * n + q], y, ls, AO.add))
             push("oMs", "aM%d_%d" % (s + 1, k), [("oI", s + 1, k), ("oT", s + 1, k), ("oy", s + 1, k)])
+            op("v", [("DS", s, k), ("N", s, k)], [("wo", s, k)],
+               tt(T.wo[:, 12 * s + c:12 * s + c + q], xb(k, 1, 2 * n + q, 2 * n + 2 * q), ls, AO.mult), [(k, 1)])
+        else:
+            op("v", [("DS", s, k), yk], [("y", k)], tt(T.Ry[:, c:c + q], y, ls, AO.add))
 
     def tail(s):
         ks = range(K)
         wo, ou = T.wo[:, 12 * s:12 * s + 12], T.ou[:, 12 * s:12 * s + 12]
-        op("v", [("w", s, k) for k in ks] + [("DS", s, k) for k in ks], [("wo", s)],
-           tt(wo, T.wp[:, 0:12], T.DS[:, s * M + 15:s * M + M:16], AO.mult), ["wp"])
-        op("v", [("wo", s), "cd"], [("wo", s)], tt(wo, wo, T.cd[:], AO.max))
+        op("v", [("wo", s, k) for k in ks] + ["cd"], [("wo", s)], tt(wo, wo, T.cd[:], AO.max))
         op("v", [("wo", s)], [("ou", s)], tc(ou, wo))
         op("v", [("ou", s)] + [("In", s, k) for k in ks], allC,
            tc(T.C[:, 0:DUMP + W].indirect(ou), T.In[:, s * M:s * M + M]))
 
-    stages = {"L": stL, "P": stP, "V": stV, "N": stN, "G": stG, "Z": stZ, "F": stF, "X": stX}
+    stages = {"L": stL, "P": stP, "V": stV, "S": stS, "N": stN, "G": stG, "R": stR, "Z": stZ, "F": stF, "X": stX,
+              "T": tail}
 
     for k in range(K):
         first(k)
         if k == 0:
             stL(0, 0)
-            op("v", ["gaps"], ["gapf"], tc(T.gapf[:], T.gaps[:]))
-    wait("g", [wrote["gapf"]])
-    rid, pid = topo.addr(way[1], core)
-    g.remote_dma(T.gapL[:], T.gapf[:], sem.agap, sem.ls, pid, rid, topo.mask(core, way[1]))
-    sent[0] += nbits(topo.mask(core, way[1]))
-    for s in range(ST):
-        for st in ORDER:
-            if s == 0 and st == "L0":
-                continue
-            stages[st[0]](s, int(st[1:]))
-        if s < ST - 1:
-            tail(s)
-    yk = [("y", ST - 1, k) for k in range(K)]
-    yp = T.wp[:, 16:28]
-    op("v", yk, ["oFq"], ts(T.oFq[:], yp, 8.0, AO.is_ge, -8.0, AO.mult), ["wp"])
-    op("v", yk + ["oFq"], ["oFy"], tt(T.oFy[:], yp, T.oFq[:], AO.add), ["wp"])
+            for kk in range(K):
+                op("v", ["gaps"], [("gb", kk)],
+                   tc(T.GB[:, GO[kk]:GO[kk] + SIZES[kk]], T.gaps[:, OFF[kk]:OFF[kk] + SIZES[kk]]))
+    push("GB", "agap1", [(x, k) for x in ("gb", "b5", "b188") for k in range(K)], GW)
+    landed("GB1", "agap1")
+    push("GB", "agap2", ["GB1"], GW)
+    for t in ORDER:
+        if t != "0L0":
+            stages[t[1]](int(t[0]), *[int(x) for x in t[2:]])
+    yk = [("y", k) for k in range(K)]
+    op("v", yk, ["oFq"], ts(T.oFq[:], T.Ry[:], 8.0, AO.is_ge, -8.0, AO.mult))
+    op("v", yk + ["oFq"], ["oFy"], tt(T.oFy[:], T.Ry[:], T.oFq[:], AO.add))
     push("oFy", "aFy", ["oFy"])
 
     total = 0

from concourse.mybir import AluOpType, ActivationFunctionType

M, B, H, ST, W = 192, 8, 5, 3, 1536
SIZES = [96, 96]
K = len(SIZES)
OFF = [sum(SIZES[:k]) for k in range(K)]
DUMP = M
BIG = 2048.0
CB = 4096.0
HALF = -(H - 0.5) / 16.0
VL0 = [48, 0]
VL = [48, 0]
VG = [0, 0]
ORDER = """
0L0 0P0 0V01 0V02 0V00 0S0 0N0 0L1 0P1 0V10 0V11 0G0 0R0 0V12 0Z0 0S1 0F0 0X0 0N1 0G1 0R1 0Z1 0F1 1L0 1P0 0X1 0T
1V01 1V00 1V02 1N0 1L1 1P1 1S0 1V10 1V11 1V12 1S1 1N1 1G0 1R0 1G1 1R1 1Z0 1F0 1X0 1Z1 1F1 1X1 2L0 2P0 1T
2V01 2V02 2V00 2N0 2L1 2R0 2P1 2S0 2V10 2G0 2V11 2V12 2S1 2N1 2G1 2Z0 2F0 2R1 2Z1 2X0 2F1 2X1
""".split()

E = 16 * M
MW = [2 * n + n // 16 for n in SIZES]
MO = [sum(MW[:k]) for k in range(K)]
MT = sum(MW)
GO = [OFF[k] + OFF[k] // 8 for k in range(K)]
GW = M + M // 8
NM = max(SIZES)
SCRATCH = {
    "C": ("sbuf", [128, DUMP + W], "int32"),
    "L": ("sbuf", [128, W], "int32"),
    "cus": ("sbuf", [128, 12], "int32"),
    "gaps": ("sbuf", [128, M], "int32"),
    "GB": ("sbuf", [128, ST * GW], "float16"),
    "RM": ("sbuf", [128, 16 * NM], "bfloat16"),
    "EX": ("sbuf", [128, 512], "float16"),
    "ID": ("sbuf", [128, 128], "float16"),
    "N4": ("sbuf", [128, 128], "float16"),
    "NI": ("sbuf", [128, 128], "float16"),
    "BP": ("sbuf", [128, 128], "float16"),
    "BN": ("sbuf", [128, 128], "float16"),
    "HB": ("sbuf", [128, 2 * NM], "float16"),
    "DM": ("sbuf", [128, M], "float32"),
    "i1": ("sbuf", [128, 512], "int32"),
    "i2": ("sbuf", [128, 128], "int32"),
    "i3": ("sbuf", [128, 128], "int32"),
    "i4": ("sbuf", [128, M], "int32"),
    "i5": ("sbuf", [128, 12], "int32"),
    "i6": ("sbuf", [128, 12], "int32"),
    "b8": ("sbuf", [128, 12], "float32"),
    "cd": ("sbuf", [128, 12], "float32"),
    "I0f": ("sbuf", [128, 12], "float32"),
    "I0u": ("sbuf", [128, 12], "uint16"),
    "cuf": ("sbuf", [128, 12], "float16"),
    "Io0": ("sbuf", [128, M], "float16"),
    "J0": ("sbuf", [128, M], "uint16"),
    "wo": ("sbuf", [128, 12 * ST], "float32"),
    "ou": ("sbuf", [128, 12 * ST], "uint16"),
    "sg": ("sbuf", [128, 24 * ST], "float16"),
    "Ru": ("sbuf", [128, 12 * ST], "uint16"),
    "Ry": ("sbuf", [128, 12], "float32"),
    "Fy": ("sbuf", [128, 12], "float32"),
    "oFy": ("sbuf", [128, 12], "float32"),
    "oFq": ("sbuf", [128, 12], "float32"),
    "J": ("sbuf", [128, ST * M], "uint16"),
    "oJ": ("sbuf", [128, ST * M], "uint16"),
    "Ms": ("sbuf", [128, ST * MT], "float16"),
    "oMs": ("sbuf", [128, ST * MT], "float16"),
    "F": ("sbuf", [128, M], "float32"),
    "oF": ("sbuf", [128, M], "float32"),
    "tT": ("sbuf", [128, ST * K * 128], "float16"),
    "xp": ("psum", [128, E], "float32"),
    "tp": ("psum", [128, 512], "float32"),
}
for _n in ("A", "P", "V", "S", "BB", "Z"):
    SCRATCH[_n] = ("sbuf", [128, ST * E], "float16")
for _n, _d in (("su", "uint16"), ("RR", "float16"), ("In", "float16"), ("GE", "float16"),
               ("m1", "float16"), ("DD", "float16"), ("DS", "float16")):
    SCRATCH[_n] = ("sbuf", [128, ST * M], _d)
SEMAPHORES = ["v", "a", "p", "gq", "ls", "lcu", "lck0", "lck1", "lla", "lgap", "agap1", "agap2", "aFy", "st"]
for _k in range(K):
    for _s in range(1, ST):
        SEMAPHORES += ["aJ%d_%d" % (_s, _k), "aM%d_%d" % (_s, _k)]
    SEMAPHORES += ["aF%d" % _k]

MSG = {"agap1": ("GB", GW, 2 * GW, 1), "agap2": ("GB", 2 * GW, 3 * GW, 1), "aFy": ("Fy", 0, 12, 1)}
for _k in range(K):
    for _s in range(1, ST):
        MSG["aJ%d_%d" % (_s, _k)] = ("J", _s * M + OFF[_k], _s * M + OFF[_k] + SIZES[_k], 0)
        MSG["aM%d_%d" % (_s, _k)] = ("Ms", _s * MT + MO[_k], _s * MT + MO[_k] + MW[_k], 1)
    MSG["aF%d" % _k] = ("F", OFF[_k], OFF[_k] + SIZES[_k], 0)
ISSUE = ["agap1", "agap2"]
for _t in ORDER:
    if _t[1] == "F":
        ISSUE.append("aJ%d_%s" % (int(_t[0]) + 1, _t[2]) if int(_t[0]) < ST - 1 else "aF" + _t[2])
    if _t[1] == "X" and int(_t[0]) < ST - 1:
        ISSUE.append("aM%d_%s" % (int(_t[0]) + 1, _t[2]))
ISSUE.append("aFy")


def lanes(topo, cores, src, dst):
    if topo.may_write(src, dst):
        return [dst, dst]
    own = [c for c in topo.cores_of(src) if c not in cores and topo.may_write(c, dst)]
    own.sort(key=lambda c: (topo.die(c) != topo.die(src), c))
    return [own[0], own[1 % len(own)]]


def nbits(m):
    return bin(m).count("1")


def rank_program(g, core, T, topo):
    cores = list(T.cores)
    n_ranks = len(cores)
    sem = T.sem
    rank = T.rank_of(core)

    def send(dst, src_name, sname, back=0):
        name, c0, c1 = MSG[sname][:3]
        rid, pid = topo.addr(dst, core)
        m = topo.mask(core, dst)
        g.remote_dma(T[name][:, c0:c1], T[src_name][:, c0 - back:c1 - back], sem[sname], sem.ls, pid, rid, m)
        return nbits(m)

    if rank is None:
        total = 0
        for r in range(n_ranks):
            src, dst = cores[r], cores[(r + 1) % n_ranks]
            way = lanes(topo, cores, src, dst)
            if core not in way:
                continue
            for sname in ISSUE:
                name, c0, c1, lane = MSG[sname]
                if way[lane] == core:
                    g.wait_ge(sem[sname], nbits(topo.mask(src, core)))
                    total += send(dst, name, sname)
        if total:
            g.wait_ge(sem.ls, total)
        return

    nxt, prv = cores[(rank + 1) % n_ranks], cores[(rank - 1) % n_ranks]
    way = lanes(topo, cores, core, nxt)
    inway = lanes(topo, cores, prv, core)
    arrives = [nbits(topo.mask(prv if w == core else w, core)) for w in inway]
    sent = [0]

    queues = {"v": (g.vector, "v"), "a": (g.scalar, "a"), "p": (g.tensor, "p"), "g": (g, "gq"), "s": (g.sync, "st")}
    count = {q: 0 for q in queues}
    seen = {q: {} for q in queues}
    wrote, readers, banks = {}, {}, {}

    def wait(q, deps):
        need = {}
        for s, val in deps:
            need[s] = max(need.get(s, 0), val)
        for s in sorted(need):
            if seen[q].get(s, 0) < need[s]:
                queues[q][0].wait_ge(sem[s], need[s])
                seen[q][s] = need[s]

    def op(q, R, Wk, call, bank=()):
        d = [wrote[k] for k in R if k in wrote]
        for k in Wk:
            if k in wrote:
                d.append(wrote[k])
            d += readers.get(k, [])
        for b in bank:
            d += [t for qq, t in banks.get(b, {}).items() if qq != q]
        wait(q, d)
        s = queues[q][1]
        call().then_inc(sem[s], 1)
        count[q] += 1
        tok = (s, count[q])
        for k in R:
            readers.setdefault(k, []).append(tok)
        for k in Wk:
            wrote[k] = tok
            readers[k] = []
        for b in bank:
            banks.setdefault(b, {})[q] = tok

    def load(eng, name, s, out, in_):
        eng.dma_start(out, in_).then_inc(sem[s], 16)
        wrote[name] = (s, 16)

    def push(src_name, sname, R, back=0):
        wait("g", [wrote[k] for k in R])
        sent[0] += send(way[MSG[sname][3]], src_name, sname, back)

    def landed(name, sname):
        wrote[name] = (sname, arrives[MSG[sname][3]])

    AO, AF = AluOpType, ActivationFunctionType
    v, te, sc = g.vector, g.tensor, g.scalar

    def ts(out, in0, s1, o0, s2=None, o1=None):
        if o1 is None:
            return lambda: v.tensor_scalar(out, in0, s1, None, o0)
        return lambda: v.tensor_scalar(out, in0, s1, s2, o0, o1)

    def tt(out, a, b, o):
        return lambda: v.tensor_tensor(out, a, b, o)

    def tc(out, in_):
        return lambda: v.tensor_copy(out, in_)

    def mm(out, lhsT, rhs, start=True, stop=True):
        return lambda: te.matmul(out, lhsT, rhs, start, stop)

    def scan(out, mask, data):
        return lambda: v.tensor_tensor_scan(out, mask, data, 0.0, AO.mult, AO.max)

    def act(out, in_):
        return lambda: sc.activation(out, in_, AF.Copy)

    n0 = 8 * SIZES[0]
    load(g.scalar, "cus", "lcu", T.cus[:], T.cu[:])
    load(g.sync, ("C", 0), "lck0", T.C[:, DUMP:DUMP + n0], T.ck[:, 0:n0])
    load(g.sync, "L", "lla", T.L[:], T.la[:])
    load(g.sync, "gaps", "lgap", T.gaps[:], T.gap[:])
    load(g.sync, ("C", 1), "lck1", T.C[:, DUMP + n0:DUMP + W], T.ck[:, n0:W])

    op("g", [], ["i5"], lambda: g.iota(T.i5[:], [[0, 12]], 0, 8))
    op("g", [], ["i6"], lambda: g.iota(T.i6[:], [[128, 12]], 0, 0))
    op("g", [], ["i2"], lambda: g.iota(T.i2[:], [[1, 128]], 0, -1))
    op("g", [], ["i1"], lambda: g.iota(T.i1[:], [[1, 512]], 0, -16))
    op("g", [], ["i3"], lambda: g.iota(T.i3[:], [[16, 8], [0, 16]], 15, -1))
    op("g", [], ["i4"], lambda: g.iota(T.i4[:], [[1, M]], 0, -1))

    op("v", ["i5"], ["i5"], ts(T.i5[:], T.i5[:], 127, AO.bitwise_and))
    op("v", [], ["RM"], lambda: v.memset(T.RM[:], 1.0))
    op("v", ["i5", "i6"], ["b8"], tt(T.b8[:], T.i5[:], T.i6[:], AO.add))
    op("v", [], ["RM"], lambda: v.memset(T.RM[:, 0:16 * NM:16], 0.0))
    op("v", ["b8", "cus"], ["I0f"], tt(T.I0f[:], T.b8[:], T.cus[:], AO.add))
    op("v", ["I0f"], ["I0u"], tc(T.I0u[:], T.I0f[:]))
    op("v", ["cus"], ["cuf"], tc(T.cuf[:], T.cus[:]))
    op("v", ["i2"], ["ID"], ts(T.ID[:], T.i2[:], 0.0, AO.is_equal))
    op("v", ["i2"], ["NI"], ts(T.NI[:], T.i2[:], 0.0, AO.is_equal, -BIG, AO.mult))
    op("v", ["i1"], ["i1"], ts(T.i1[:], T.i1[:], 511, AO.bitwise_and))
    op("v", ["i3"], ["i3"], ts(T.i3[:], T.i3[:], 4, AO.arith_shift_right))
    op("v", ["i4"], ["i4"], ts(T.i4[:], T.i4[:], 15, AO.bitwise_and))
    op("v", ["i1"], ["EX"], ts(T.EX[:], T.i1[:], 16.0, AO.is_lt, BIG, AO.mult))
    op("v", ["i2"], ["N4"], ts(T.N4[:], T.i2[:], 0.0, AO.is_equal, -4.0, AO.mult))
    op("v", ["i3"], ["BP"], ts(T.BP[:], T.i3[:], 0.0, AO.is_equal, CB, AO.mult))
    op("v", ["i3"], ["BN"], ts(T.BN[:], T.i3[:], 0.0, AO.is_equal, -CB, AO.mult))
    op("v", ["i2"], ["HB0"], ts(T.HB[:, 0:NM], T.i2[:, 0:NM], 0.0, AO.mult, HALF, AO.add))
    op("v", ["i2"], ["HB1"], ts(T.HB[:, NM:2 * NM], T.i2[:, 0:NM], 0.0, AO.mult, -HALF, AO.add))
    op("v", ["i4"], ["DM"], ts(T.DM[:], T.i4[:], 0.0, AO.is_gt, 1.0e6, AO.mult))
    for k in range(K):
        q, c = SIZES[k] // 16, OFF[k] // 16
        o = GO[k] + SIZES[k]
        op("v", ["b8"], [("b5", k)], ts(T.GB[:, o:o + q], T.b8[:, c:c + q], -3.0, AO.add))
        op("v", ["b8"], [("b188", k)], ts(T.GB[:, o + q:o + 2 * q], T.b8[:, c:c + q], float(DUMP - 4), AO.add))
    op("v", ["b8"], ["cd"], ts(T.cd[:], T.b8[:], 0.125, AO.mult))

    allC = [("C", 0), ("C", 1)]

    def cl(s, k):
        return s * 12 + OFF[k] // 16, s * 12 + (OFF[k] + SIZES[k]) // 16

    def sl(name, s, k):
        return T[name][:, s * M + OFF[k]:s * M + OFF[k] + SIZES[k]]

    def big(name, s, k, a=0, b=None):
        o = s * E + 16 * OFF[k]
        return T[name][:, o + 16 * a:o + 16 * (SIZES[k] if b is None else b)]

    def lasts(name, s, k):
        o = s * E + 16 * OFF[k]
        return T[name][:, o + 15:o + 16 * SIZES[k]:16]

    def xb(k, m, a, b):
        o = 16 * OFF[k] + 512 * m
        return T.xp[:, o + a:o + b]

    def ideal(s, k):
        n = SIZES[k]
        if s == 0:
            return T.Io0[:, OFF[k]:OFF[k] + n], ("Io", k)
        o = s * MT + MO[k]
        return T.Ms[:, o:o + n], ("M", s, k)

    def base(s, k):
        n = SIZES[k]
        if s == 0:
            return ideal(0, k)
        o = s * MT + MO[k] + n
        return T.Ms[:, o:o + n], ("M", s, k)

    def place(s, k):
        n = SIZES[k]
        if s == 0:
            return T.cuf[:, OFF[k] // 16:(OFF[k] + n) // 16], "cuf"
        o = s * MT + MO[k] + 2 * n
        return T.Ms[:, o:o + n // 16], ("M", s, k)

    def gather(q, R, Wk, out, win, off):
        if q == "v":
            op("v", R, Wk, tc(out, win.indirect(off)))
        else:
            op("a", R, Wk, act(out, win.indirect(off)))

    def first(k):
        o, n = OFF[k], SIZES[k]
        keys = [("C", 0)] if k == 0 else allC
        gather("a", ["I0u"] + keys, [("Io", k)], T.Io0[:, o:o + n], T.C[:, DUMP:DUMP + 8 * (o + n)],
               T.I0u[:, o // 16:(o + n) // 16])
        op("v", [("Io", k)], [("J", 0, k)], tc(T.J0[:, o:o + n], T.Io0[:, o:o + n]))

    def stL(s, k):
        n = SIZES[k]
        if s == 0:
            J, j0 = T.J0, OFF[k]
        else:
            landed(("J", s, k), "aJ%d_%d" % (s, k))
            J, j0 = T.J, s * M + OFF[k]
        nv = (VL0 if s == 0 else VL)[k]
        na = n - nv
        if na:
            gather("a", [("J", s, k), "L"], [("A", s, k, 0)], big("A", s, k, 0, na), T.L[:], J[:, j0:j0 + na])
        if nv:
            gather("v", [("J", s, k), "L"], [("A", s, k, 1)], big("A", s, k, na, n), T.L[:], J[:, j0 + na:j0 + n])

    def akeys(s, k):
        return [("A", s, k, 0), ("A", s, k, 1)]

    def stP(s, k):
        n = SIZES[k]
        op("v", akeys(s, k) + ["RM"], [("P", s, k)], scan(big("P", s, k), T.RM[:, 0:16 * n], big("A", s, k)))
        for m in range(n // 32):
            op("p", akeys(s, k) + ["NI"], [("X", s, k, m)],
               mm(xb(k, m, 0, 512), T.NI[:], big("A", s, k, 32 * m, 32 * m + 32), True, False), [(k, m)])
        op("p", [("P", s, k), "ID"], [("tp", s, k)], mm(T.tp[0:n, 0:128], lasts("P", s, k), T.ID[:]), ["tp"])
        o = 128 * (s * K + k)
        op("a", [("tp", s, k)], [("tT", s, k)], act(T.tT[0:n, o:o + 128], T.tp[0:n, 0:128]), ["tp"])
        for m in range(n // 32):
            op("p", [("tT", s, k), "EX"], [("X", s, k, m)],
               mm(xb(k, m, 0, 512), T.tT[32 * m:32 * m + 32, o:o + 128], T.EX[32 * m:32 * m + 32, :], False, True),
               [(k, m)])

    def stV(s, k, m):
        op("v", akeys(s, k) + [("X", s, k, m)], [("V", s, k, m)],
           tt(big("V", s, k, 32 * m, 32 * m + 32), xb(k, m, 0, 512), big("A", s, k, 32 * m, 32 * m + 32), AO.min),
           [(k, m)])

    def stS(s, k):
        n = SIZES[k]
        op("v", [("V", s, k, m) for m in range(n // 32)] + ["RM"], [("S", s, k)],
           scan(big("S", s, k), T.RM[:, 0:16 * n], big("V", s, k)))
        op("v", [("S", s, k)], [("su", s, k)], tc(sl("su", s, k), lasts("S", s, k)))

    def stN(s, k):
        n = SIZES[k]
        q = n // 16
        c0, c1 = cl(s, k)
        if s > 0:
            landed(("M", s, k), "aM%d_%d" % (s, k))
        y, yk = place(s, k)
        o = 24 * s + OFF[k] // 8
        op("a", [yk], [("sg", s, k)], lambda: sc.activation(T.sg[:, o:o + q], y, AF.Sign, bias=-6.5))
        op("a", [yk], [("sh", s, k)], lambda: sc.activation(T.sg[:, o + q:o + 2 * q], y, AF.Sign, bias=-7.5))
        b = [(k, 1)]
        p0 = 2 * n
        N = ("N", s, k)
        if s == 0:
            I, ik = ideal(s, k)
            gk = ("gb", k)
            op("p", [ik, "ID"], [N], mm(xb(k, 1, 0, n), T.ID[:], I, True, False), b)
            op("p", [ik, "ID"], [N], mm(xb(k, 1, n, p0), T.ID[:], I, False, False), b)
            op("p", [yk, "ID"], [N], mm(xb(k, 1, p0, p0 + q), T.ID[:], y, False, False), b)
        else:
            m = s * MT + MO[k]
            gk = "GB%d" % s
            if gk not in wrote:
                landed(gk, "agap%d" % s)
            op("p", [yk, "ID"], [N], mm(xb(k, 1, 0, p0 + q), T.ID[:], T.Ms[:, m:m + p0 + q], True, False), b)
        op("p", [yk, "ID"], [N], mm(xb(k, 1, p0 + q, p0 + 2 * q), T.ID[:], y, False, False), b)
        gs = s * GW + GO[k]
        op("p", [gk, ("b5", k), ("b188", k)], [N],
           mm(xb(k, 1, n, p0 + 2 * q), T.ID[:], T.GB[:, gs:gs + n + 2 * q], False, False), b)
        op("p", [("sg", s, k), ("sh", s, k), "N4"], [N],
           mm(xb(k, 1, p0, p0 + 2 * q), T.N4[:], T.sg[:, o:o + 2 * q], False, True), b)
        op("v", [N], [("Ru", s, k)], tc(T.Ru[:, c0:c1], xb(k, 1, p0, p0 + q)), b)

    def stG(s, k):
        n = SIZES[k]
        nv = VG[k]
        na = n - nv
        win = T.C[:, DUMP:DUMP + W]
        o = s * M + OFF[k]
        if na:
            gather("a", [("su", s, k)] + allC, [("B", s, k, 0)], big("BB", s, k, 0, na), win, T.su[:, o:o + na])
        if nv:
            gather("v", [("su", s, k)] + allC, [("B", s, k, 1)], big("BB", s, k, na, n), win, T.su[:, o + na:o + n])

    def stR(s, k):
        c0, c1 = cl(s, k)
        gather("a", [("Ru", s, k)] + allC, [("RR", s, k)], sl("RR", s, k), T.C[:, DUMP:DUMP + W], T.Ru[:, c0:c1])

    def stZ(s, k):
        n = SIZES[k]
        In, GE = sl("In", s, k), sl("GE", s, k)
        op("v", [("B", s, k, 0), ("B", s, k, 1), "RM"], [("Z", s, k)],
           scan(big("Z", s, k), T.RM[:, 0:16 * n], big("BB", s, k)))
        op("v", [("Z", s, k), ("N", s, k)], [("In", s, k)], tt(In, xb(k, 1, 0, n), lasts("Z", s, k), AO.max), [(k, 1)])
        op("v", [("In", s, k), ("N", s, k)], [("GE", s, k)], tt(GE, In, xb(k, 1, n, 2 * n), AO.is_ge), [(k, 1)])
        b = [(k, 0)]
        op("p", ["BP", "HB0", "HB1"], [("+", s, k)],
           mm(xb(k, 0, 0, 2 * n), T.BP[:], T.HB[:, NM - n:NM + n], True, False), b)
        op("p", [("GE", s, k)], [("+", s, k)], mm(xb(k, 0, 0, n), T.BP[:], GE, False, False), b)
        op("p", [("GE", s, k), "BN"], [("+", s, k)], mm(xb(k, 0, n, 2 * n), T.BN[:], GE, False, True), b)

    def stF(s, k):
        n = SIZES[k]
        if s < ST - 1:
            o = (s + 1) * MT + MO[k]
            out, key = T.oMs[:, o:o + n], ("oI", s + 1, k)
        else:
            out, key = T.oF[:, OFF[k]:OFF[k] + n], ("oF", k)
        b = [(k, 0)]
        m1, m2 = sl("m1", s, k), xb(k, 0, 2 * n, 3 * n)
        op("v", [("+", s, k), ("RR", s, k)], [("m1", s, k)], tt(m1, xb(k, 0, 0, n), sl("RR", s, k), AO.min), b)
        op("v", [("+", s, k), ("In", s, k)], [("m2", s, k)], tt(m2, xb(k, 0, n, 2 * n), sl("In", s, k), AO.min), b)
        op("v", [("m1", s, k), ("m2", s, k)], [key], tt(out, m2, m1, AO.max), b)
        if s < ST - 1:
            op("v", [key], [("oJ", s + 1, k)], tc(sl("oJ", s + 1, k), out))
            push("oJ", "aJ%d_%d" % (s + 1, k), [("oJ", s + 1, k)])
        else:
            push("oF", "aF%d" % k, [key])

    def stX(s, k):
        n = SIZES[k]
        q = n // 16
        c = OFF[k] // 16
        D, DS = sl("DD", s, k), sl("DS", s, k)
        b0 = [(k, 0)]
        op("v", [("+", s, k), "DM"], [("DD", s, k)], tt(D, xb(k, 0, 0, n), T.DM[:, OFF[k]:OFF[k] + n], AO.is_ge), b0)
        if s < ST - 1:
            o = (s + 1) * MT + MO[k]
            m2 = xb(k, 0, 3 * n, 4 * n)
            t, tk = base(s, k)
            op("v", [("+", s, k), tk], [("m3", s, k)], tt(m2, xb(k, 0, n, 2 * n), t, AO.min), b0)
        op("v", [("DD", s, k), "RM"], [("DS", s, k)], scan(DS, T.RM[:, 0:n], D))
        if s < ST - 1:
            op("v", [("m3", s, k), ("m1", s, k)], [("oT", s + 1, k)],
               tt(T.oMs[:, o + n:o + 2 * n], m2, sl("m1", s, k), AO.max), b0)
        y, yk = place(s, k)
        os = s * M + OFF[k]
        ls = T.DS[:, os + 15:os + n:16]
        if s < ST - 1:
            op("v", [("DS", s, k), yk], [("oy", s + 1, k)], tt(T.oMs[:, o + 2 * n:o + 2 * n + q], y, ls, AO.add))
            push("oMs", "aM%d_%d" % (s + 1, k), [("oI", s + 1, k), ("oT", s + 1, k), ("oy", s + 1, k)])
            op("v", [("DS", s, k), ("N", s, k)], [("wo", s, k)],
               tt(T.wo[:, 12 * s + c:12 * s + c + q], xb(k, 1, 2 * n + q, 2 * n + 2 * q), ls, AO.mult), [(k, 1)])
        else:
            op("v", [("DS", s, k), yk], [("y", k)], tt(T.Ry[:, c:c + q], y, ls, AO.add))

    def tail(s):
        ks = range(K)
        wo, ou = T.wo[:, 12 * s:12 * s + 12], T.ou[:, 12 * s:12 * s + 12]
        op("v", [("wo", s, k) for k in ks] + ["cd"], [("wo", s)], tt(wo, wo, T.cd[:], AO.max))
        op("v", [("wo", s)], [("ou", s)], tc(ou, wo))
        op("v", [("ou", s)] + [("In", s, k) for k in ks], allC,
           tc(T.C[:, 0:DUMP + W].indirect(ou), T.In[:, s * M:s * M + M]))

    stages = {"L": stL, "P": stP, "V": stV, "S": stS, "N": stN, "G": stG, "R": stR, "Z": stZ, "F": stF, "X": stX,
              "T": tail}

    for k in range(K):
        first(k)
        if k == 0:
            stL(0, 0)
            for kk in range(K):
                op("v", ["gaps"], [("gb", kk)],
                   tc(T.GB[:, GO[kk]:GO[kk] + SIZES[kk]], T.gaps[:, OFF[kk]:OFF[kk] + SIZES[kk]]))
    push("GB", "agap1", [(x, k) for x in ("gb", "b5", "b188") for k in range(K)], GW)
    landed("GB1", "agap1")
    push("GB", "agap2", ["GB1"], GW)
    for t in ORDER:
        if t != "0L0":
            stages[t[1]](int(t[0]), *[int(x) for x in t[2:]])
    yk = [("y", k) for k in range(K)]
    op("v", yk, ["oFq"], ts(T.oFq[:], T.Ry[:], 8.0, AO.is_ge, -8.0, AO.mult))
    op("v", yk + ["oFq"], ["oFy"], tt(T.oFy[:], T.Ry[:], T.oFq[:], AO.add))
    push("oFy", "aFy", ["oFy"])

    total = 0
    for k in range(K):
        landed(("F", k), "aF%d" % k)
        wait("s", [wrote[("F", k)]])
        g.sync.dma_start(T.yi[:, OFF[k]:OFF[k] + SIZES[k]], T.F[:, OFF[k]:OFF[k] + SIZES[k]]).then_inc(sem.st, 16)
        total += 16
    landed("Fy", "aFy")
    wait("s", [wrote["Fy"]])
    g.sync.dma_start(T.yc[:], T.Fy[:]).then_inc(sem.st, 16)
    total += 16
    g.sync.wait_ge(sem.st, total)
    g.wait_ge(sem.ls, sent[0])
    for q, s in (("v", "v"), ("a", "a"), ("p", "p"), ("g", "gq")):
        g.wait_ge(sem[s], count[q])
